import numpy as np
import ml_dtypes


def mxq(x, axis, fmt="e4m3"):
    dtype, down = {"e4m3": (ml_dtypes.float8_e4m3fn, 7), "e5m2": (ml_dtypes.float8_e5m2, 14)}[fmt]
    v = np.moveaxis(np.asarray(x, np.float32).astype(ml_dtypes.bfloat16).astype(np.float64), axis, -1)
    blocks = v.reshape(v.shape[:-1] + (-1, 32))
    amax = np.abs(blocks).max(-1, keepdims=True)
    byte = np.maximum(np.where(amax > 0, np.frexp(amax)[1] - 1 + 127, 0) - down, 1)
    scale = np.exp2(byte - 127.0)
    codes = (blocks / scale).astype(np.float32).astype(dtype).astype(np.float64)
    return np.moveaxis((codes * scale).reshape(v.shape), -1, axis)


WIDE = False


def mx_kscale(k):
    if not WIDE:
        return np.ones(k)
    levels = np.array([10, -10, 5, -5, 0])
    if k % 512:
        return np.exp2(np.random.permutation(np.resize(levels, k // 32))).repeat(32)
    a = np.empty((k // 512, 16))
    for p in range(k // 512):
        a[p, :8] = np.random.permutation(np.resize(levels, 8))
        for g in range(8):
            far = levels[np.abs(levels - a[p, g]) >= 10]
            a[p, g + 8] = far[np.random.randint(len(far))]
    return np.exp2(a.ravel()).repeat(32)


def f64(x):
    return np.asarray(x).astype(np.float64)


def striped(idx):
    return np.tile(idx.reshape(-1, 16).T, (8, 1)).astype(np.uint16)


def unstriped(offs):
    return offs[:16].T.reshape(-1).astype(np.int64)


E2M1 = np.array([0.0, 0.5, 1.0, 1.5, 2.0, 3.0, 4.0, 6.0, -0.0, -0.5, -1.0, -1.5, -2.0, -3.0, -4.0, -6.0])


def pack_weight(w, fmt):
    k, n = w.shape
    w = f64(np.asarray(w, np.float32).astype(ml_dtypes.bfloat16)).reshape(k // 32, 32, n)
    amax = np.abs(w).max(1)
    if fmt == "e4m3":
        byte = np.frexp(amax)[1] - 1 + 127 - 7
    else:
        mant, ex = np.frexp(amax / 6.0)
        byte = np.where(mant > 0.5, ex, ex - 1) + 127
    byte = np.clip(np.where(amax > 0, byte, 1), 1, 254)
    scaled = (w * np.exp2(127.0 - byte)[:, None, :]).reshape(k, n).astype(np.float32)
    by_word = np.ascontiguousarray(scaled.reshape(k // 512, 128, 4, n).transpose(0, 1, 3, 2))
    if fmt == "e4m3":
        words = by_word.astype(ml_dtypes.float8_e4m3fn).view(np.uint8)
    else:
        c = by_word.astype(ml_dtypes.float4_e2m1fn).view(np.uint8) & 0xF
        words = (c[..., 0::2] | (c[..., 1::2] << 4)).reshape(k // 512, 128, 2 * n)
    return np.ascontiguousarray(words), np.ascontiguousarray(byte.astype(np.uint8).reshape(k // 512, 16, n))


def unpack_weight(words, scales, fmt):
    g, _, n = scales.shape
    words = np.ascontiguousarray(words).reshape(g, 128, n, -1)
    if fmt == "e4m3":
        vals = words.view(ml_dtypes.float8_e4m3fn).astype(np.float64)
    else:
        nib = np.empty((g, 128, n, 4), np.uint8)
        nib[..., 0::2] = words & 0xF
        nib[..., 1::2] = words >> 4
        vals = E2M1[nib]
    vals = vals * np.repeat(np.exp2(scales.astype(np.float64) - 127.0), 8, axis=1)[..., None]
    return vals.transpose(0, 1, 3, 2).reshape(g * 512, n)


K, T, E, C, N = 2560, 640, 6, 128, 256
R = 4


def by_expert(wq, xq):
    return np.concatenate([wq[e].T @ xq[:, e * C:(e + 1) * C] for e in range(E)], axis=1)


def setup_inputs():
    n = np.random.standard_normal
    s = mx_kscale(K)[:, None]
    slot_token = np.concatenate([r * (T // R) + np.random.permutation(T // R)[:C // R] for e in range(E) for r in range(R)])
    w = [pack_weight(m, "e2m1") for m in n((E, K, N)) / np.sqrt(K) / s[None]]
    return {
        "xT": (n((K, T)) * s).astype(np.float32),
        "w_words": np.stack([m[0] for m in w]),
        "w_scales": np.stack([m[1] for m in w]),
        "offs": striped(slot_token),
    }


def reference(xT, w_words, w_scales, offs):
    idx = unstriped(offs)
    w = np.stack([unpack_weight(w_words[e], w_scales[e], "e2m1") for e in range(E)])
    xq = mxq(f64(xT)[:, idx], 0, "e4m3")
    y = by_expert(w, xq)
    return y.reshape(N, E, R, C // R).transpose(0, 2, 1, 3).reshape(N, E * C)

@@ -1,0 +1,157 @@
+from contextlib import ExitStack
+
+import concourse.mybir as mybir
+
+K, T, E, C, N = 2560, 640, 6, 128, 256
+R = 4
+S = E * C
+P = 128
+A = K // 512
+U = C // R
+
+F32 = mybir.dt.float32
+BF16 = mybir.dt.bfloat16
+I32 = mybir.dt.int32
+U32 = mybir.dt.uint32
+U16 = mybir.dt.uint16
+U8 = mybir.dt.uint8
+FP8X4 = mybir.dt.float8_e4m3fn_x4
+FP4X4 = mybir.dt.float4_e2m1fn_x4
+
+FLOPS = 2 * K * N * S
+
+WINDOW = 1024
+FIRST_ROW = [4, 8, 12, 0]
+SCALAR_COLS = [224, 320, 448, 512, 384]
+SHIFT_ROWS = 112
+
+
+def tile_moe_eps_lin_none_kernel(tc, xT, w_words, w_scales, offs, out):
+    nc = tc.nc
+    with ExitStack() as ctx:
+        keep = ctx.enter_context(tc.tile_pool(name="keep", bufs=1))
+        psum = ctx.enter_context(tc.psum_pool(name="psum", bufs=8))
+
+        offsets = keep.tile([P, S // 16], U16, name="offsets")
+        raw = [keep.tile([P, 4, T], F32, name=f"raw{a}") for a in range(A)]
+        grouped = [keep.tile([P, T * 4], BF16, name=f"grouped{a}", align_bytes=64) for a in range(A)]
+        codes = [keep.tile([P, WINDOW], I32, name=f"codes{a}", align_bytes=64) for a in range(A)]
+        packed = keep.tile([P, WINDOW], U8, name="packed", align_bytes=64)
+        single = keep.tile([P, WINDOW], U8, name="single", align_bytes=64)
+        slot_words = [keep.tile([P, S], I32, name=f"slot_words{a}", align_bytes=64) for a in range(A)]
+        slot_packed = keep.tile([P, S], U8, name="slot_packed", align_bytes=64)
+        slot_single = keep.tile([P, S], U8, name="slot_single", align_bytes=64)
+        shifted = [keep.tile([P, S], U8, name=f"shifted{a}", align_bytes=64) for a in range(3)]
+        weights = [keep.tile([P, A * 2 * N], U8, name=f"weights{e}", align_bytes=64) for e in range(E)]
+        w_planes = keep.tile([P, E * A * N], U8, name="w_planes", align_bytes=64)
+        result = [keep.tile([P, S], F32, name=f"result{h}") for h in range(2)]
+
+        for a in range(A):
+            nc.sync.dma_start(out=raw[a][:], in_=xT[512 * a : 512 * (a + 1), :].rearrange("(p j) t -> p j t", j=4))
+            if a == 0:
+                nc.sync.dma_start(offsets[:], offs)
+        nc.vector.memset(w_planes[:].bitcast(I32), 0)
+        for q in range(4):
+            nc.gpsimd.dma_start(
+                out=w_planes[32 * q : 32 * q + 4, :].bitcast(I32).rearrange("q (g n) -> q g n", g=E * A),
+                in_=w_scales[:, :, 4 * q : 4 * q + 4, :].bitcast(I32).rearrange("e a q n -> q (e a) n"),
+            )
+        for a in range(A):
+            nc.vector.memset(codes[a][:, T:WINDOW], 0)
+        nc.gpsimd.memset(packed[:], 0)
+        nc.gpsimd.memset(single[:], 0)
+        for a in range(3):
+            nc.gpsimd.memset(shifted[a][:], 0)
+        for e in range(E):
+            nc.sync.dma_start(
+                out=weights[e][:].bitcast(I32).rearrange("p (a n) -> p a n", a=A),
+                in_=w_words[e].bitcast(I32).rearrange("a p n -> p a n"),
+            )
+
+        def interleave(a, engine_copy, lo, hi):
+            engine_copy(
+                out=grouped[a][:, 4 * lo : 4 * hi].rearrange("p (c i j) -> p c j i", i=4, j=4),
+                in_=raw[a][:, :, lo:hi].rearrange("p j (c i) -> p c j i", i=4),
+            )
+
+        def quantise(a, lo, hi):
+            if a < 4:
+                plane = packed[FIRST_ROW[a] : P, lo:hi]
+            else:
+                plane = single[:, lo:hi]
+            nc.vector.quantize_mx(out=codes[a][:, lo:hi].bitcast(FP8X4), scales=plane, in_=grouped[a][:, 4 * lo : 4 * hi])
+
+        def gather_words(a, lo, hi):
+            nc.vector.tensor_copy(
+                slot_words[a][:, lo:hi].bitcast(U32),
+                codes[a][:].bitcast(U32).indirect(offsets[:, lo // 16 : hi // 16]),
+            )
+
+        def gather_bytes(dst, src, lo, hi):
+            nc.vector.tensor_copy(dst[:, lo:hi], src[:].indirect(offsets[:, lo // 16 : hi // 16]))
+
+        for a in range(A):
+            cut = SCALAR_COLS[a]
+            interleave(a, nc.scalar.copy, 0, cut)
+            interleave(a, nc.vector.tensor_copy, cut, T)
+            quantise(a, 0, 512)
+            quantise(a, 512, T)
+            if a == 3:
+                gather_bytes(slot_packed, packed, 0, S)
+                for b in range(3):
+                    first = FIRST_ROW[b]
+                    nc.scalar.dma_start(
+                        out=shifted[b][0:SHIFT_ROWS, :].bitcast(I32),
+                        in_=slot_packed[first : first + SHIFT_ROWS, :].bitcast(I32),
+                    )
+            if a < 4:
+                gather_words(a, 0, S)
+            else:
+                for lo, hi in ((0, 512), (512, S)):
+                    gather_bytes(slot_single, single, lo, hi)
+                    gather_words(a, lo, hi)
+
+        planes = shifted + [slot_packed, slot_single]
+        accs = {}
+
+        def multiply(e, h, a, start, stop):
+            words = weights[e][:, 512 * a + 256 * h : 512 * a + 256 * h + 256]
+            g = (e * A + a) * N + 128 * h
+            slots = slice(C * e, C * (e + 1))
+            nc.tensor.matmul_mx(
+                out=accs[e, h][:],
+                lhsT=words.bitcast(FP4X4),
+                lhsT_scale=w_planes[:, g : g + 128],
+                rhs=slot_words[a][:, slots].bitcast(FP8X4),
+                rhs_scale=planes[a][:, slots],
+                start=start,
+                stop=stop,
+            )
+
+        def leave(e, h, engine_copy):
+            engine_copy(
+                out=result[h][:].rearrange("p (m e u) -> p m e u", m=R, e=E)[:, :, e, :],
+                in_=accs[e, h][:].rearrange("p (m u) -> p m u", m=R),
+            )
+
+        for e in range(4):
+            for h in range(2):
+                accs[e, h] = psum.tile([P, C], F32, name="acc")
+                multiply(e, h, 3, True, False)
+        for e in range(4):
+            for a in range(3):
+                for h in range(2):
+                    multiply(e, h, a, False, False)
+        for e in range(4):
+            for h in range(2):
+                multiply(e, h, 4, False, True)
+                leave(e, h, nc.scalar.copy)
+        for e in (4, 5):
+            for h in range(2):
+                accs[e, h] = psum.tile([P, C], F32, name="acc")
+                for i, a in enumerate((3, 0, 1, 2, 4)):
+                    multiply(e, h, a, i == 0, i == 4)
+            leave(e, 0, nc.scalar.copy)
+            leave(e, 1, nc.vector.tensor_copy)
+        nc.sync.dma_start(out=out[0:P, :], in_=result[0][:])
+        nc.scalar.dma_start(out=out[P : 2 * P, :], in_=result[1][:])

@@ -22,7 +22,7 @@ FLOPS = 2 * K * N * S
 
 WINDOW = 1024
 FIRST_ROW = [4, 8, 12, 0]
-SCALAR_COLS = [224, 320, 448, 512, 384]
+SCALAR_COLS = [224, 384, 512, 544, 576]
 SHIFT_ROWS = 112
 
 
@@ -35,9 +35,9 @@ def tile_moe_eps_lin_none_kernel(tc, xT, w_words, w_scales, offs, out):
         offsets = keep.tile([P, S // 16], U16, name="offsets")
         raw = [keep.tile([P, 4, T], F32, name=f"raw{a}") for a in range(A)]
         grouped = [keep.tile([P, T * 4], BF16, name=f"grouped{a}", align_bytes=64) for a in range(A)]
-        codes = [keep.tile([P, WINDOW], I32, name=f"codes{a}", align_bytes=64) for a in range(A)]
+        codes = [keep.tile([P, T], I32, name=f"codes{a}", align_bytes=64) for a in range(A)]
         packed = keep.tile([P, WINDOW], U8, name="packed", align_bytes=64)
-        single = keep.tile([P, WINDOW], U8, name="single", align_bytes=64)
+        single = keep.tile([P, T], U8, name="single", align_bytes=64)
         slot_words = [keep.tile([P, S], I32, name=f"slot_words{a}", align_bytes=64) for a in range(A)]
         slot_packed = keep.tile([P, S], U8, name="slot_packed", align_bytes=64)
         slot_single = keep.tile([P, S], U8, name="slot_single", align_bytes=64)
@@ -50,18 +50,16 @@ def tile_moe_eps_lin_none_kernel(tc, xT, w_words, w_scales, offs, out):
             nc.sync.dma_start(out=raw[a][:], in_=xT[512 * a : 512 * (a + 1), :].rearrange("(p j) t -> p j t", j=4))
             if a == 0:
                 nc.sync.dma_start(offsets[:], offs)
-        nc.vector.memset(w_planes[:].bitcast(I32), 0)
-        for q in range(4):
-            nc.gpsimd.dma_start(
-                out=w_planes[32 * q : 32 * q + 4, :].bitcast(I32).rearrange("q (g n) -> q g n", g=E * A),
-                in_=w_scales[:, :, 4 * q : 4 * q + 4, :].bitcast(I32).rearrange("e a q n -> q (e a) n"),
+        nc.gpsimd.memset(w_planes[:].bitcast(I32), 0)
+        for r in range(4):
+            nc.sync.dma_start(
+                out=w_planes[r:P:32, :].bitcast(I32).rearrange("q (g n) -> q g n", g=E * A),
+                in_=w_scales[:, :, r:16:4, :].bitcast(I32).rearrange("e a q n -> q (e a) n"),
             )
-        for a in range(A):
-            nc.vector.memset(codes[a][:, T:WINDOW], 0)
-        nc.gpsimd.memset(packed[:], 0)
-        nc.gpsimd.memset(single[:], 0)
+        nc.vector.memset(packed[:].bitcast(I32), 0)
+        nc.vector.memset(single[:].bitcast(I32), 0)
         for a in range(3):
-            nc.gpsimd.memset(shifted[a][:], 0)
+            nc.gpsimd.memset(shifted[a][:].bitcast(I32), 0)
         for e in range(E):
             nc.sync.dma_start(
                 out=weights[e][:].bitcast(I32).rearrange("p (a n) -> p a n", a=A),
@@ -92,24 +90,28 @@ def tile_moe_eps_lin_none_kernel(tc, xT, w_words, w_scales, offs, out):
 
         for a in range(A):
             cut = SCALAR_COLS[a]
-            interleave(a, nc.scalar.copy, 0, cut)
-            interleave(a, nc.vector.tensor_copy, cut, T)
-            quantise(a, 0, 512)
-            quantise(a, 512, T)
-            if a == 3:
-                gather_bytes(slot_packed, packed, 0, S)
+            mid = 320 if a == 4 else cut
+            interleave(a, nc.scalar.copy, 0, mid)
+            if a == 4:
                 for b in range(3):
                     first = FIRST_ROW[b]
                     nc.scalar.dma_start(
                         out=shifted[b][0:SHIFT_ROWS, :].bitcast(I32),
                         in_=slot_packed[first : first + SHIFT_ROWS, :].bitcast(I32),
                     )
+                interleave(a, nc.scalar.copy, mid, cut)
+            interleave(a, nc.vector.tensor_copy, cut, T)
+            quantise(a, 0, 512)
+            quantise(a, 512, T)
+            if a > 0:
+                gather_words(a - 1, 480, S)
+            if a == 3:
+                gather_bytes(slot_packed, packed, 0, S)
             if a < 4:
-                gather_words(a, 0, S)
-            else:
-                for lo, hi in ((0, 512), (512, S)):
-                    gather_bytes(slot_single, single, lo, hi)
-                    gather_words(a, lo, hi)
+                gather_words(a, 0, 480)
+        for lo in (0, 256, 512):
+            gather_bytes(slot_single, single, lo, lo + 256)
+            gather_words(4, lo, lo + 256)
 
         planes = shifted + [slot_packed, slot_single]
         accs = {}
@@ -142,15 +144,22 @@ def tile_moe_eps_lin_none_kernel(tc, xT, w_words, w_scales, offs, out):
             for a in range(3):
                 for h in range(2):
                     multiply(e, h, a, False, False)
-        for e in range(4):
+        for e in (0, 1):
             for h in range(2):
                 multiply(e, h, 4, False, True)
                 leave(e, h, nc.scalar.copy)
         for e in (4, 5):
             for h in range(2):
                 accs[e, h] = psum.tile([P, C], F32, name="acc")
-                for i, a in enumerate((3, 0, 1, 2, 4)):
-                    multiply(e, h, a, i == 0, i == 4)
+                for a in (3, 0, 1, 2):
+                    multiply(e, h, a, a == 3, False)
+        for e in (2, 3):
+            for h in range(2):
+                multiply(e, h, 4, False, True)
+                leave(e, h, nc.scalar.copy)
+        for e in (4, 5):
+            for h in range(2):
+                multiply(e, h, 4, False, True)
             leave(e, 0, nc.scalar.copy)
             leave(e, 1, nc.vector.tensor_copy)
         nc.sync.dma_start(out=out[0:P, :], in_=result[0][:])

from contextlib import ExitStack

import concourse.mybir as mybir

K, T, E, C, N = 2560, 640, 6, 128, 256
R = 4
S = E * C
P = 128
A = K // 512
U = C // R

F32 = mybir.dt.float32
BF16 = mybir.dt.bfloat16
I32 = mybir.dt.int32
U32 = mybir.dt.uint32
U16 = mybir.dt.uint16
U8 = mybir.dt.uint8
FP8X4 = mybir.dt.float8_e4m3fn_x4
FP4X4 = mybir.dt.float4_e2m1fn_x4

FLOPS = 2 * K * N * S

WINDOW = 1024
FIRST_ROW = [4, 8, 12, 0]
SCALAR_COLS = [224, 384, 512, 544, 576]
SHIFT_ROWS = 112


def tile_moe_eps_lin_none_kernel(tc, xT, w_words, w_scales, offs, out):
    nc = tc.nc
    with ExitStack() as ctx:
        keep = ctx.enter_context(tc.tile_pool(name="keep", bufs=1))
        psum = ctx.enter_context(tc.psum_pool(name="psum", bufs=8))

        offsets = keep.tile([P, S // 16], U16, name="offsets")
        raw = [keep.tile([P, 4, T], F32, name=f"raw{a}") for a in range(A)]
        grouped = [keep.tile([P, T * 4], BF16, name=f"grouped{a}", align_bytes=64) for a in range(A)]
        codes = [keep.tile([P, T], I32, name=f"codes{a}", align_bytes=64) for a in range(A)]
        packed = keep.tile([P, WINDOW], U8, name="packed", align_bytes=64)
        single = keep.tile([P, T], U8, name="single", align_bytes=64)
        slot_words = [keep.tile([P, S], I32, name=f"slot_words{a}", align_bytes=64) for a in range(A)]
        slot_packed = keep.tile([P, S], U8, name="slot_packed", align_bytes=64)
        slot_single = keep.tile([P, S], U8, name="slot_single", align_bytes=64)
        shifted = [keep.tile([P, S], U8, name=f"shifted{a}", align_bytes=64) for a in range(3)]
        weights = [keep.tile([P, A * 2 * N], U8, name=f"weights{e}", align_bytes=64) for e in range(E)]
        w_planes = keep.tile([P, E * A * N], U8, name="w_planes", align_bytes=64)
        result = [keep.tile([P, S], F32, name=f"result{h}") for h in range(2)]

        for a in range(A):
            nc.sync.dma_start(out=raw[a][:], in_=xT[512 * a : 512 * (a + 1), :].rearrange("(p j) t -> p j t", j=4))
            if a == 0:
                nc.sync.dma_start(offsets[:], offs)
        nc.gpsimd.memset(w_planes[:].bitcast(I32), 0)
        for r in range(4):
            nc.sync.dma_start(
                out=w_planes[r:P:32, :].bitcast(I32).rearrange("q (g n) -> q g n", g=E * A),
                in_=w_scales[:, :, r:16:4, :].bitcast(I32).rearrange("e a q n -> q (e a) n"),
            )
        nc.vector.memset(packed[:].bitcast(I32), 0)
        nc.vector.memset(single[:].bitcast(I32), 0)
        for a in range(3):
            nc.gpsimd.memset(shifted[a][:].bitcast(I32), 0)
        for e in range(E):
            nc.sync.dma_start(
                out=weights[e][:].bitcast(I32).rearrange("p (a n) -> p a n", a=A),
                in_=w_words[e].bitcast(I32).rearrange("a p n -> p a n"),
            )

        def interleave(a, engine_copy, lo, hi):
            engine_copy(
                out=grouped[a][:, 4 * lo : 4 * hi].rearrange("p (c i j) -> p c j i", i=4, j=4),
                in_=raw[a][:, :, lo:hi].rearrange("p j (c i) -> p c j i", i=4),
            )

        def quantise(a, lo, hi):
            if a < 4:
                plane = packed[FIRST_ROW[a] : P, lo:hi]
            else:
                plane = single[:, lo:hi]
            nc.vector.quantize_mx(out=codes[a][:, lo:hi].bitcast(FP8X4), scales=plane, in_=grouped[a][:, 4 * lo : 4 * hi])

        def gather_words(a, lo, hi):
            nc.vector.tensor_copy(
                slot_words[a][:, lo:hi].bitcast(U32),
                codes[a][:].bitcast(U32).indirect(offsets[:, lo // 16 : hi // 16]),
            )

        def gather_bytes(dst, src, lo, hi):
            nc.vector.tensor_copy(dst[:, lo:hi], src[:].indirect(offsets[:, lo // 16 : hi // 16]))

        for a in range(A):
            cut = SCALAR_COLS[a]
            mid = 320 if a == 4 else cut
            interleave(a, nc.scalar.copy, 0, mid)
            if a == 4:
                for b in range(3):
                    first = FIRST_ROW[b]
                    nc.scalar.dma_start(
                        out=shifted[b][0:SHIFT_ROWS, :].bitcast(I32),
                        in_=slot_packed[first : first + SHIFT_ROWS, :].bitcast(I32),
                    )
                interleave(a, nc.scalar.copy, mid, cut)
            interleave(a, nc.vector.tensor_copy, cut, T)
            quantise(a, 0, 512)
            quantise(a, 512, T)
            if a > 0:
                gather_words(a - 1, 480, S)
            if a == 3:
                gather_bytes(slot_packed, packed, 0, S)
            if a < 4:
                gather_words(a, 0, 480)
        for lo in (0, 256, 512):
            gather_bytes(slot_single, single, lo, lo + 256)
            gather_words(4, lo, lo + 256)

        planes = shifted + [slot_packed, slot_single]
        accs = {}

        def multiply(e, h, a, start, stop):
            words = weights[e][:, 512 * a + 256 * h : 512 * a + 256 * h + 256]
            g = (e * A + a) * N + 128 * h
            slots = slice(C * e, C * (e + 1))
            nc.tensor.matmul_mx(
                out=accs[e, h][:],
                lhsT=words.bitcast(FP4X4),
                lhsT_scale=w_planes[:, g : g + 128],
                rhs=slot_words[a][:, slots].bitcast(FP8X4),
                rhs_scale=planes[a][:, slots],
                start=start,
                stop=stop,
            )

        def leave(e, h, engine_copy):
            engine_copy(
                out=result[h][:].rearrange("p (m e u) -> p m e u", m=R, e=E)[:, :, e, :],
                in_=accs[e, h][:].rearrange("p (m u) -> p m u", m=R),
            )

        for e in range(4):
            for h in range(2):
                accs[e, h] = psum.tile([P, C], F32, name="acc")
                multiply(e, h, 3, True, False)
        for e in range(4):
            for a in range(3):
                for h in range(2):
                    multiply(e, h, a, False, False)
        for e in (0, 1):
            for h in range(2):
                multiply(e, h, 4, False, True)
                leave(e, h, nc.scalar.copy)
        for e in (4, 5):
            for h in range(2):
                accs[e, h] = psum.tile([P, C], F32, name="acc")
                for a in (3, 0, 1, 2):
                    multiply(e, h, a, a == 3, False)
        for e in (2, 3):
            for h in range(2):
                multiply(e, h, 4, False, True)
                leave(e, h, nc.scalar.copy)
        for e in (4, 5):
            for h in range(2):
                multiply(e, h, 4, False, True)
            leave(e, 0, nc.scalar.copy)
            leave(e, 1, nc.vector.tensor_copy)
        nc.sync.dma_start(out=out[0:P, :], in_=result[0][:])
        nc.scalar.dma_start(out=out[P : 2 * P, :], in_=result[1][:])
